import numpy as np
import ml_dtypes


def mxq(x, axis, fmt="e4m3"):
    dtype, down = {"e4m3": (ml_dtypes.float8_e4m3fn, 7), "e5m2": (ml_dtypes.float8_e5m2, 14)}[fmt]
    v = np.moveaxis(np.asarray(x, np.float32).astype(ml_dtypes.bfloat16).astype(np.float64), axis, -1)
    blocks = v.reshape(v.shape[:-1] + (-1, 32))
    amax = np.abs(blocks).max(-1, keepdims=True)
    byte = np.maximum(np.where(amax > 0, np.frexp(amax)[1] - 1 + 127, 0) - down, 1)
    scale = np.exp2(byte - 127.0)
    codes = (blocks / scale).astype(np.float32).astype(dtype).astype(np.float64)
    return np.moveaxis((codes * scale).reshape(v.shape), -1, axis)


WIDE = False


def mx_kscale(k):
    if not WIDE:
        return np.ones(k)
    levels = np.array([10, -10, 5, -5, 0])
    if k % 512:
        return np.exp2(np.random.permutation(np.resize(levels, k // 32))).repeat(32)
    a = np.empty((k // 512, 16))
    for p in range(k // 512):
        a[p, :8] = np.random.permutation(np.resize(levels, 8))
        for g in range(8):
            far = levels[np.abs(levels - a[p, g]) >= 10]
            a[p, g + 8] = far[np.random.randint(len(far))]
    return np.exp2(a.ravel()).repeat(32)


def f64(x):
    return np.asarray(x).astype(np.float64)


def striped(idx):
    return np.tile(idx.reshape(-1, 16).T, (8, 1)).astype(np.uint16)


def unstriped(offs):
    return offs[:16].T.reshape(-1).astype(np.int64)


E2M1 = np.array([0.0, 0.5, 1.0, 1.5, 2.0, 3.0, 4.0, 6.0, -0.0, -0.5, -1.0, -1.5, -2.0, -3.0, -4.0, -6.0])


def pack_weight(w, fmt):
    k, n = w.shape
    w = f64(np.asarray(w, np.float32).astype(ml_dtypes.bfloat16)).reshape(k // 32, 32, n)
    amax = np.abs(w).max(1)
    if fmt == "e4m3":
        byte = np.frexp(amax)[1] - 1 + 127 - 7
    else:
        mant, ex = np.frexp(amax / 6.0)
        byte = np.where(mant > 0.5, ex, ex - 1) + 127
    byte = np.clip(np.where(amax > 0, byte, 1), 1, 254)
    scaled = (w * np.exp2(127.0 - byte)[:, None, :]).reshape(k, n).astype(np.float32)
    by_word = np.ascontiguousarray(scaled.reshape(k // 512, 128, 4, n).transpose(0, 1, 3, 2))
    if fmt == "e4m3":
        words = by_word.astype(ml_dtypes.float8_e4m3fn).view(np.uint8)
    else:
        c = by_word.astype(ml_dtypes.float4_e2m1fn).view(np.uint8) & 0xF
        words = (c[..., 0::2] | (c[..., 1::2] << 4)).reshape(k // 512, 128, 2 * n)
    return np.ascontiguousarray(words), np.ascontiguousarray(byte.astype(np.uint8).reshape(k // 512, 16, n))


def unpack_weight(words, scales, fmt):
    g, _, n = scales.shape
    words = np.ascontiguousarray(words).reshape(g, 128, n, -1)
    if fmt == "e4m3":
        vals = words.view(ml_dtypes.float8_e4m3fn).astype(np.float64)
    else:
        nib = np.empty((g, 128, n, 4), np.uint8)
        nib[..., 0::2] = words & 0xF
        nib[..., 1::2] = words >> 4
        vals = E2M1[nib]
    vals = vals * np.repeat(np.exp2(scales.astype(np.float64) - 127.0), 8, axis=1)[..., None]
    return vals.transpose(0, 1, 3, 2).reshape(g * 512, n)


def gelu(v):
    return 0.5 * v * (1.0 + np.tanh(np.sqrt(2.0 / np.pi) * (v + 0.044715 * v**3)))


def twice(P):
    return np.random.permutation(np.repeat(np.arange(P), 2))


K, H, T, S, P = 1024, 1024, 4096, 1024, 512

def setup_inputs():
    n = np.random.standard_normal
    s = mx_kscale(K)[:, None]
    u = mx_kscale(H)[:, None]
    d = {}
    d["tab_words"], d["tab_scales"] = pack_weight(n((K, T)) * s, "e4m3")
    d["offs"] = striped(np.random.permutation(T)[:S])
    d["w1"] = (n((K, H)) / K ** 0.5 / s * u.T).astype(np.float32)
    d["rest"] = (0.7 * n((H, S)) * u).astype(np.float32)
    d["pos1"] = striped(np.random.permutation(S)[:P])
    d["pos2"] = striped(np.random.permutation(S)[:P])
    d["w4_words"], d["w4_scales"] = pack_weight(1.3 * n((H, H)) / H ** 0.5 / u, "e2m1")
    d["pos3"] = striped(twice(P))
    d["gain"] = (0.5 * np.exp(0.3 * n(H)) / u[:, 0]).astype(np.float32)
    return d

def reference(tab_words, tab_scales, offs, w1, rest, pos1, pos2, w4_words, w4_scales, pos3, gain):
    v = unpack_weight(tab_words, tab_scales, "e4m3")[:, unstriped(offs)]
    h = (mxq(f64(w1), 0, "e4m3").T @ v) + f64(rest)
    x = np.minimum(h[:, unstriped(pos1)], h[:, unstriped(pos2)])
    w4 = unpack_weight(w4_words, w4_scales, "e2m1")
    y = w4.T @ mxq(x, 0, "e4m3")
    up = y[:, unstriped(pos3)]
    return up / (1.0 + np.abs(up)) + f64(gain)[:, None] * h

@@ -1,0 +1,236 @@
+from contextlib import ExitStack
+
+import concourse.mybir as mybir
+
+K, H, T, S, PAIRS = 1024, 1024, 4096, 1024, 512
+FLOPS = 2 * K * H * S + 2 * H * H * PAIRS
+
+F32 = mybir.dt.float32
+BF16 = mybir.dt.bfloat16
+I32 = mybir.dt.int32
+U32 = mybir.dt.uint32
+U16 = mybir.dt.uint16
+U8 = mybir.dt.uint8
+FP8X4 = mybir.dt.float8_e4m3fn_x4
+FP4X4 = mybir.dt.float4_e2m1fn_x4
+ALU = mybir.AluOpType
+ACT = mybir.ActivationFunctionType
+
+P = 128
+PACK = 4
+PASS = P * PACK
+BANK = 512
+HALF = PAIRS // 2
+SPARE = 16
+
+
+def tile_list_polygraph_arousal_scorer_kernel(
+    tc, tab_words, tab_scales, offs, w1, rest, pos1, pos2, w4_words, w4_scales, pos3, gain, out
+):
+    nc = tc.nc
+    with ExitStack() as ctx:
+        keep = ctx.enter_context(tc.tile_pool(name="keep", bufs=1))
+        ring2 = ctx.enter_context(tc.tile_pool(name="ring2", bufs=2))
+        ring3 = ctx.enter_context(tc.tile_pool(name="ring3", bufs=3))
+        psum = ctx.enter_context(tc.psum_pool(name="psum", bufs=1))
+
+        offs_t = keep.tile([P, S // 16], U16, name="offs_t")
+        pos1_t = keep.tile([P, PAIRS // 16], U16, name="pos1_t")
+        pos2_t = keep.tile([P, PAIRS // 16], U16, name="pos2_t")
+        pos3_t = keep.tile([P, S // 16], U16, name="pos3_t")
+        gain_t = keep.tile([P, 2, PACK], F32, name="gain_t")
+        warm = keep.tile([P, 2], F32, name="warm")
+
+        w4w_raw = keep.tile([P, 2 * 2 * H], U8, name="w4w_raw", align_bytes=64)
+        w4s_raw = keep.tile([P, 2 * H], U8, name="w4s_raw", align_bytes=64)
+        w4w = keep.tile([P, 2 * 2 * H], U8, name="w4w", align_bytes=64)
+        w4s = keep.tile([P, 2 * H], U8, name="w4s", align_bytes=64)
+        tabw = [keep.tile([P, T], I32, name="tabw%d" % a, align_bytes=64) for a in range(2)]
+        tabs = keep.tile([P, T], U8, name="tabs", align_bytes=64)
+        vw = [keep.tile([P, S], U32, name="vw%d" % a, align_bytes=64) for a in range(2)]
+        vs = keep.tile([P, S], U8, name="vs", align_bytes=64)
+        w1raw = {}
+        w1c = {}
+        w1s = {}
+        for b in range(2):
+            for a in range(2):
+                w1raw[a, b] = keep.tile([P, PACK, PASS], F32, name="w1raw%d%d" % (a, b))
+                w1c[a, b] = keep.tile([P, PASS], U32, name="w1c%d%d" % (a, b), align_bytes=64)
+                w1s[a, b] = keep.tile([P, PASS], U8, name="w1s%d%d" % (a, b), align_bytes=64)
+        rest_t = [keep.tile([P, S], F32, name="rest%d" % i) for i in range(8)]
+        h_t = [keep.tile([P, S], F32, name="h%d" % i) for i in range(8)]
+        g1 = keep.tile([P, PACK, PAIRS], F32, name="g1")
+        g2 = keep.tile([P, PACK, PAIRS], F32, name="g2")
+        xc = [keep.tile([P, PAIRS], U32, name="xc%d" % b, align_bytes=64) for b in range(2)]
+        xs = [keep.tile([P, PAIRS], U8, name="xs%d" % b, align_bytes=64) for b in range(2)]
+        win = [keep.tile([P, PAIRS + SPARE], F32, name="win%d" % i) for i in range(8)]
+
+        nc.vector.memset(w4s_raw[:].bitcast(I32), 0)
+        nc.vector.memset(tabs[:].bitcast(I32), 0)
+        for i in range(8):
+            nc.gpsimd.memset(win[i][:, PAIRS:], 0.0)
+        nc.gpsimd.memset(warm[:, 0:1], 1.0)
+        nc.scalar.activation(warm[:, 1:2], warm[:, 0:1], ACT.Abs_reciprocal_sqrt)
+
+        def load_w1(a, b):
+            nc.sync.dma_start(
+                w1raw[a, b][:],
+                w1[PASS * a : PASS * (a + 1), PASS * b : PASS * (b + 1)].rearrange("(p j) c -> p j c", j=PACK),
+            )
+
+        def load_rest(i):
+            b, t = divmod(i, PACK)
+            rows = rest[PASS * b : PASS * (b + 1), :].rearrange("(p t) j -> t p j", t=PACK)
+            nc.sync.dma_start(rest_t[i][:], rows[t])
+
+        def load_tab(a):
+            nc.sync.dma_start(tabw[a][:], tab_words[a].rearrange("p n i -> p (n i)").bitcast(I32))
+
+        nc.sync.dma_start(
+            w4w_raw[:].bitcast(I32).rearrange("p (a n) -> p a n", a=2),
+            w4_words.bitcast(I32).rearrange("a p n -> p a n"),
+        )
+        nc.sync.dma_start(offs_t[:], offs)
+        load_tab(0)
+        w4s_src = w4_scales.bitcast(I32).rearrange("a (q r) n -> r q a n", r=4)
+        w4s_dst = w4s_raw[:].bitcast(I32).rearrange("p (a n) -> p a n", a=2)
+        for r in range(4):
+            nc.sync.dma_start(w4s_dst[r:P:32], w4s_src[r])
+        tabs_src = tab_scales.bitcast(I32)
+        tabs_dst = tabs[:].bitcast(I32)
+        for q in range(4):
+            nc.sync.dma_start(tabs_dst[32 * q : 32 * q + 8, :], tabs_src[:, 4 * q : 4 * q + 4, :])
+        load_tab(1)
+        load_w1(0, 0)
+        load_w1(1, 0)
+        load_rest(0)
+        nc.sync.dma_start(pos1_t[:], pos1)
+        nc.sync.dma_start(pos2_t[:], pos2)
+        load_rest(1)
+        load_rest(2)
+        load_rest(3)
+        nc.sync.dma_start(gain_t[:], gain.rearrange("(b p t) -> p b t", b=2, t=PACK))
+        load_w1(0, 1)
+        load_w1(1, 1)
+        for i in range(4, 8):
+            load_rest(i)
+        nc.sync.dma_start(pos3_t[:], pos3)
+
+        nc.vector.tensor_copy(
+            w4w[:].rearrange("p (g t q e) -> p g q t e", g=4, t=PACK, e=2),
+            w4w_raw[:].rearrange("p (g q t e) -> p g q t e", g=4, t=PACK, e=2),
+        )
+        nc.vector.tensor_copy(
+            w4s[:].rearrange("p (g t q) -> p g q t", g=4, t=PACK),
+            w4s_raw[:].rearrange("p (g q t) -> p g q t", g=4, t=PACK),
+        )
+
+        def gather_words(a):
+            nc.vector.tensor_copy(vw[a][:], tabw[a][:].bitcast(U32).indirect(offs_t[:]))
+
+        def quantize_w1(a, b):
+            grouped = ring2.tile([P, PASS * PACK], BF16, name="grouped", align_bytes=64)
+            nc.scalar.copy(
+                grouped[:].rearrange("p (t m j) -> p m j t", t=PACK, j=PACK),
+                w1raw[a, b][:].rearrange("p j (m t) -> p m j t", t=PACK),
+            )
+            nc.vector.quantize_mx(w1c[a, b][:].bitcast(FP8X4), w1s[a, b][:], grouped[:])
+
+        def make_h(i):
+            b, t = divmod(i, PACK)
+            cols = slice(P * t, P * (t + 1))
+            for u in range(2):
+                acc = psum.tile([P, BANK], F32, name="acc", tag="bank%d" % ((2 * i + u) % 8))
+                js = slice(BANK * u, BANK * (u + 1))
+                for a in range(2):
+                    nc.tensor.matmul_mx(
+                        acc[:],
+                        lhsT=w1c[a, b][:, cols].bitcast(FP8X4),
+                        lhsT_scale=w1s[a, b][:, cols],
+                        rhs=vw[a][:, js].bitcast(FP8X4),
+                        rhs_scale=vs[4 * a : P, js],
+                        start=(a == 0),
+                        stop=(a == 1),
+                    )
+                nc.vector.tensor_tensor(h_t[i][:, js], acc[:], rest_t[i][:, js], ALU.add)
+            nc.scalar.activation(rest_t[i][:], h_t[i][:], ACT.Copy, scale=gain_t[:, b, t : t + 1])
+
+        def gather_pairs(i, m0, m1):
+            t = i % PACK
+            ls = slice(m0 // 16, m1 // 16)
+            nc.vector.tensor_copy(g1[:, t, m0:m1], h_t[i][:].indirect(pos1_t[:, ls]))
+            nc.vector.tensor_copy(g2[:, t, m0:m1], h_t[i][:].indirect(pos2_t[:, ls]))
+
+        def make_x(b, m0, m1):
+            n = m1 - m0
+            xi = keep.tile([P, n * PACK], BF16, name="xi", tag="xi%d_%d" % (b, m0), align_bytes=64)
+            nc.vector.tensor_tensor(
+                xi[:].rearrange("p (c i t) -> p c t i", t=PACK, i=4),
+                g1[:, :, m0:m1].rearrange("p t (c i) -> p c t i", i=4),
+                g2[:, :, m0:m1].rearrange("p t (c i) -> p c t i", i=4),
+                ALU.min,
+            )
+            nc.vector.quantize_mx(xc[b][:, m0:m1].bitcast(FP8X4), xs[b][:, m0:m1], xi[:])
+
+        def scores(half, pair):
+            acc = psum.tile([P, 2, HALF], F32, name="acc2", tag="bank%d" % (4 * half + pair))
+            for v in range(2):
+                i = 2 * pair + v
+                for c in range(HALF // P):
+                    ms = slice(HALF * half + P * c, HALF * half + P * (c + 1))
+                    for a in range(2):
+                        col = H * a + P * i
+                        nc.tensor.matmul_mx(
+                            acc[:, v, P * c : P * (c + 1)],
+                            lhsT=w4w[:, 2 * col : 2 * (col + P)].bitcast(FP4X4),
+                            lhsT_scale=w4s[:, col : col + P],
+                            rhs=xc[a][:, ms].bitcast(FP8X4),
+                            rhs_scale=xs[a][:, ms],
+                            start=(a == 0),
+                            stop=(a == 1),
+                        )
+            mag = ring2.tile([P, 2, HALF], F32, name="mag")
+            root = ring2.tile([P, 2, HALF], F32, name="root")
+            inv = ring3.tile([P, 2, HALF], F32, name="inv")
+            nc.scalar.activation(mag[:], acc[:], ACT.Abs)
+            nc.scalar.activation(root[:], mag[:], ACT.Abs_reciprocal_sqrt, bias=1.0)
+            nc.scalar.activation(inv[:], root[:], ACT.Square)
+            for v in range(2):
+                i = 2 * pair + v
+                nc.vector.tensor_tensor(win[i][:, HALF * half : HALF * (half + 1)], acc[:, v, :], inv[:, v, :], ALU.mult)
+
+        def finish(i):
+            b, t = divmod(i, PACK)
+            rows = out[PASS * b : PASS * (b + 1), :].rearrange("(p t) j -> t p j", t=PACK)
+            for u in range(2):
+                js = slice(BANK * u, BANK * (u + 1))
+                res = ring3.tile([P, BANK], F32, name="res")
+                nc.vector.tensor_tensor(
+                    res[:], win[i][:].indirect(pos3_t[:, 32 * u : 32 * (u + 1)]), rest_t[i][:, js], ALU.add
+                )
+                nc.sync.dma_start(rows[t][:, js], res[:])
+
+        gather_words(0)
+        nc.vector.tensor_copy(vs[:], tabs[:].indirect(offs_t[:]))
+        gather_words(1)
+        quantize_w1(0, 0)
+        quantize_w1(1, 0)
+        for i in range(4):
+            make_h(i)
+            gather_pairs(i, 0, PAIRS)
+        quantize_w1(0, 1)
+        quantize_w1(1, 1)
+        make_x(0, 0, PAIRS)
+        for i in range(4, 8):
+            make_h(i)
+            gather_pairs(i, 0, HALF)
+        make_x(1, 0, HALF)
+        for i in range(4, 8):
+            gather_pairs(i, HALF, PAIRS)
+        for pair in range(4):
+            scores(0, pair)
+        make_x(1, HALF, PAIRS)
+        for pair in range(4):
+            scores(1, pair)
+            finish(2 * pair)
+            finish(2 * pair + 1)

@@ -22,6 +22,8 @@ PASS = P * PACK
 BANK = 512
 HALF = PAIRS // 2
 SPARE = 16
+V_ADDS = (0, 1, 2, 3, 4, 5, 6, 7)
+V_FINAL = (0, 1, 2, 3, 4, 5, 6, 7)
 
 
 def tile_list_polygraph_arousal_scorer_kernel(
@@ -54,7 +56,8 @@ def tile_list_polygraph_arousal_scorer_kernel(
         w1s = {}
         for b in range(2):
             for a in range(2):
-                w1raw[a, b] = keep.tile([P, PACK, PASS], F32, name="w1raw%d%d" % (a, b))
+                for u in range(2):
+                    w1raw[a, b, u] = keep.tile([P, PACK, PASS // 2], F32, name="w1raw%d%d%d" % (a, b, u))
                 w1c[a, b] = keep.tile([P, PASS], U32, name="w1c%d%d" % (a, b), align_bytes=64)
                 w1s[a, b] = keep.tile([P, PASS], U8, name="w1s%d%d" % (a, b), align_bytes=64)
         rest_t = [keep.tile([P, S], F32, name="rest%d" % i) for i in range(8)]
@@ -65,18 +68,24 @@ def tile_list_polygraph_arousal_scorer_kernel(
         xs = [keep.tile([P, PAIRS], U8, name="xs%d" % b, align_bytes=64) for b in range(2)]
         win = [keep.tile([P, PAIRS + SPARE], F32, name="win%d" % i) for i in range(8)]
 
-        nc.vector.memset(w4s_raw[:].bitcast(I32), 0)
         nc.vector.memset(tabs[:].bitcast(I32), 0)
+        nc.gpsimd.memset(w4s_raw[:].bitcast(I32), 0)
+        w4s_src = w4_scales.bitcast(I32).rearrange("a (q r) n -> r q a n", r=4)
+        w4s_dst = w4s_raw[:].bitcast(I32).rearrange("p (a n) -> p a n", a=2)
+        for r in range(4):
+            nc.gpsimd.dma_start(w4s_dst[r:P:32], w4s_src[r])
+        nc.vector.memset(warm[:, 0:1], 1.0)
+        nc.scalar.activation(warm[:, 1:2], warm[:, 0:1], ACT.Abs_reciprocal_sqrt)
         for i in range(8):
             nc.gpsimd.memset(win[i][:, PAIRS:], 0.0)
-        nc.gpsimd.memset(warm[:, 0:1], 1.0)
-        nc.scalar.activation(warm[:, 1:2], warm[:, 0:1], ACT.Abs_reciprocal_sqrt)
 
         def load_w1(a, b):
-            nc.sync.dma_start(
-                w1raw[a, b][:],
-                w1[PASS * a : PASS * (a + 1), PASS * b : PASS * (b + 1)].rearrange("(p j) c -> p j c", j=PACK),
-            )
+            for u in range(2):
+                c0 = PASS * b + PASS // 2 * u
+                nc.sync.dma_start(
+                    w1raw[a, b, u][:],
+                    w1[PASS * a : PASS * (a + 1), c0 : c0 + PASS // 2].rearrange("(p j) c -> p j c", j=PACK),
+                )
 
         def load_rest(i):
             b, t = divmod(i, PACK)
@@ -90,31 +99,27 @@ def tile_list_polygraph_arousal_scorer_kernel(
             w4w_raw[:].bitcast(I32).rearrange("p (a n) -> p a n", a=2),
             w4_words.bitcast(I32).rearrange("a p n -> p a n"),
         )
-        nc.sync.dma_start(offs_t[:], offs)
         load_tab(0)
-        w4s_src = w4_scales.bitcast(I32).rearrange("a (q r) n -> r q a n", r=4)
-        w4s_dst = w4s_raw[:].bitcast(I32).rearrange("p (a n) -> p a n", a=2)
-        for r in range(4):
-            nc.sync.dma_start(w4s_dst[r:P:32], w4s_src[r])
+        nc.sync.dma_start(offs_t[:], offs)
+        nc.sync.dma_start(pos1_t[:], pos1)
+        nc.sync.dma_start(pos2_t[:], pos2)
+        nc.sync.dma_start(pos3_t[:], pos3)
+        load_w1(0, 0)
         tabs_src = tab_scales.bitcast(I32)
         tabs_dst = tabs[:].bitcast(I32)
         for q in range(4):
             nc.sync.dma_start(tabs_dst[32 * q : 32 * q + 8, :], tabs_src[:, 4 * q : 4 * q + 4, :])
         load_tab(1)
-        load_w1(0, 0)
         load_w1(1, 0)
         load_rest(0)
-        nc.sync.dma_start(pos1_t[:], pos1)
-        nc.sync.dma_start(pos2_t[:], pos2)
         load_rest(1)
+        load_w1(0, 1)
         load_rest(2)
+        load_w1(1, 1)
         load_rest(3)
         nc.sync.dma_start(gain_t[:], gain.rearrange("(b p t) -> p b t", b=2, t=PACK))
-        load_w1(0, 1)
-        load_w1(1, 1)
         for i in range(4, 8):
             load_rest(i)
-        nc.sync.dma_start(pos3_t[:], pos3)
 
         nc.vector.tensor_copy(
             w4w[:].rearrange("p (g t q e) -> p g q t e", g=4, t=PACK, e=2),
@@ -128,12 +133,11 @@ def tile_list_polygraph_arousal_scorer_kernel(
         def gather_words(a):
             nc.vector.tensor_copy(vw[a][:], tabw[a][:].bitcast(U32).indirect(offs_t[:]))
 
-        def quantize_w1(a, b):
+        def quantize_w1(a, b, copies):
             grouped = ring2.tile([P, PASS * PACK], BF16, name="grouped", align_bytes=64)
-            nc.scalar.copy(
-                grouped[:].rearrange("p (t m j) -> p m j t", t=PACK, j=PACK),
-                w1raw[a, b][:].rearrange("p j (m t) -> p m j t", t=PACK),
-            )
+            view = grouped[:].rearrange("p (t m j) -> p m j t", t=PACK, j=PACK)
+            for u in range(2):
+                copies[u](view[:, 64 * u : 64 * (u + 1)], w1raw[a, b, u][:].rearrange("p j (m t) -> p m j t", t=PACK))
             nc.vector.quantize_mx(w1c[a, b][:].bitcast(FP8X4), w1s[a, b][:], grouped[:])
 
         def make_h(i):
@@ -152,7 +156,14 @@ def tile_list_polygraph_arousal_scorer_kernel(
                         start=(a == 0),
                         stop=(a == 1),
                     )
-                nc.vector.tensor_tensor(h_t[i][:, js], acc[:], rest_t[i][:, js], ALU.add)
+                if i in V_ADDS:
+                    nc.vector.tensor_tensor(h_t[i][:, js], acc[:], rest_t[i][:, js], ALU.add)
+                else:
+                    nc.scalar.copy(h_t[i][:, js], acc[:])
+                    nc.gpsimd.tensor_tensor(h_t[i][:, js], h_t[i][:, js], rest_t[i][:, js], ALU.add)
+
+        def scale_h(i):
+            b, t = divmod(i, PACK)
             nc.scalar.activation(rest_t[i][:], h_t[i][:], ACT.Copy, scale=gain_t[:, b, t : t + 1])
 
         def gather_pairs(i, m0, m1):
@@ -204,25 +215,39 @@ def tile_list_polygraph_arousal_scorer_kernel(
             rows = out[PASS * b : PASS * (b + 1), :].rearrange("(p t) j -> t p j", t=PACK)
             for u in range(2):
                 js = slice(BANK * u, BANK * (u + 1))
-                res = ring3.tile([P, BANK], F32, name="res")
-                nc.vector.tensor_tensor(
-                    res[:], win[i][:].indirect(pos3_t[:, 32 * u : 32 * (u + 1)]), rest_t[i][:, js], ALU.add
-                )
-                nc.sync.dma_start(rows[t][:, js], res[:])
+                res = h_t[i][:, js]
+                picked = win[i][:].indirect(pos3_t[:, 32 * u : 32 * (u + 1)])
+                if i in V_FINAL:
+                    nc.vector.tensor_tensor(res, picked, rest_t[i][:, js], ALU.add)
+                    nc.sync.dma_start(rows[t][:, js], res)
+                else:
+                    nc.vector.tensor_copy(res, picked)
+                    nc.gpsimd.tensor_tensor(rest_t[i][:, js], res, rest_t[i][:, js], ALU.add)
+                    nc.sync.dma_start(rows[t][:, js], rest_t[i][:, js])
 
+        on_scalar = (nc.scalar.copy, nc.scalar.copy)
         gather_words(0)
         nc.vector.tensor_copy(vs[:], tabs[:].indirect(offs_t[:]))
+        quantize_w1(0, 0, on_scalar)
         gather_words(1)
-        quantize_w1(0, 0)
-        quantize_w1(1, 0)
-        for i in range(4):
+        quantize_w1(1, 0, (nc.scalar.copy, nc.vector.tensor_copy))
+        make_h(0)
+        make_h(1)
+        gather_pairs(0, 0, PAIRS)
+        make_h(2)
+        quantize_w1(0, 1, on_scalar)
+        gather_pairs(1, 0, PAIRS)
+        make_h(3)
+        quantize_w1(1, 1, on_scalar)
+        gather_pairs(2, 0, PAIRS)
+        for i in range(4, 7):
             make_h(i)
-            gather_pairs(i, 0, PAIRS)
-        quantize_w1(0, 1)
-        quantize_w1(1, 1)
+        gather_pairs(3, 0, PAIRS)
         make_x(0, 0, PAIRS)
+        make_h(7)
+        for i in range(4):
+            scale_h(i)
         for i in range(4, 8):
-            make_h(i)
             gather_pairs(i, 0, HALF)
         make_x(1, 0, HALF)
         for i in range(4, 8):
@@ -232,5 +257,6 @@ def tile_list_polygraph_arousal_scorer_kernel(
         make_x(1, HALF, PAIRS)
         for pair in range(4):
             scores(1, pair)
+            scale_h(4 + pair)
             finish(2 * pair)
             finish(2 * pair + 1)

@@ -22,7 +22,7 @@ PASS = P * PACK
 BANK = 512
 HALF = PAIRS // 2
 SPARE = 16
-V_ADDS = (0, 1, 2, 3, 4, 5, 6, 7)
+V_ADDS = (0, 7)
 V_FINAL = (0, 1, 2, 3, 4, 5, 6, 7)
 
 
@@ -34,6 +34,7 @@ def tile_list_polygraph_arousal_scorer_kernel(
         keep = ctx.enter_context(tc.tile_pool(name="keep", bufs=1))
         ring2 = ctx.enter_context(tc.tile_pool(name="ring2", bufs=2))
         ring3 = ctx.enter_context(tc.tile_pool(name="ring3", bufs=3))
+        shared = ctx.enter_context(tc.tile_pool(name="shared", bufs=1))
         psum = ctx.enter_context(tc.psum_pool(name="psum", bufs=1))
 
         offs_t = keep.tile([P, S // 16], U16, name="offs_t")
@@ -44,11 +45,12 @@ def tile_list_polygraph_arousal_scorer_kernel(
         warm = keep.tile([P, 2], F32, name="warm")
 
         w4w_raw = keep.tile([P, 2 * 2 * H], U8, name="w4w_raw", align_bytes=64)
-        w4s_raw = keep.tile([P, 2 * H], U8, name="w4s_raw", align_bytes=64)
-        w4w = keep.tile([P, 2 * 2 * H], U8, name="w4w", align_bytes=64)
+        w4s_raw = keep.tile([P, H], U8, name="w4s_raw", align_bytes=64)
+        w4s_dealt = keep.tile([P, H], U8, name="w4s_dealt", align_bytes=64)
         w4s = keep.tile([P, 2 * H], U8, name="w4s", align_bytes=64)
+        w4w = keep.tile([P, 2 * 2 * H], U8, name="w4w", align_bytes=64)
         tabw = [keep.tile([P, T], I32, name="tabw%d" % a, align_bytes=64) for a in range(2)]
-        tabs = keep.tile([P, T], U8, name="tabs", align_bytes=64)
+        tabs = shared.tile([P, T], U8, name="tabs", align_bytes=64, offset=0)
         vw = [keep.tile([P, S], U32, name="vw%d" % a, align_bytes=64) for a in range(2)]
         vs = keep.tile([P, S], U8, name="vs", align_bytes=64)
         w1raw = {}
@@ -56,9 +58,11 @@ def tile_list_polygraph_arousal_scorer_kernel(
         w1s = {}
         for b in range(2):
             for a in range(2):
-                for u in range(2):
-                    w1raw[a, b, u] = keep.tile([P, PACK, PASS // 2], F32, name="w1raw%d%d%d" % (a, b, u))
-                w1c[a, b] = keep.tile([P, PASS], U32, name="w1c%d%d" % (a, b), align_bytes=64)
+                w1raw[a, b] = keep.tile([P, PACK, PASS], F32, name="w1raw%d%d" % (a, b), align_bytes=64)
+                if (a, b) == (0, 0):
+                    w1c[a, b] = shared.tile([P, PASS], U32, name="w1c00", align_bytes=64, offset=2 * H)
+                else:
+                    w1c[a, b] = keep.tile([P, PASS], U32, name="w1c%d%d" % (a, b), align_bytes=64)
                 w1s[a, b] = keep.tile([P, PASS], U8, name="w1s%d%d" % (a, b), align_bytes=64)
         rest_t = [keep.tile([P, S], F32, name="rest%d" % i) for i in range(8)]
         h_t = [keep.tile([P, S], F32, name="h%d" % i) for i in range(8)]
@@ -69,23 +73,19 @@ def tile_list_polygraph_arousal_scorer_kernel(
         win = [keep.tile([P, PAIRS + SPARE], F32, name="win%d" % i) for i in range(8)]
 
         nc.vector.memset(tabs[:].bitcast(I32), 0)
-        nc.gpsimd.memset(w4s_raw[:].bitcast(I32), 0)
-        w4s_src = w4_scales.bitcast(I32).rearrange("a (q r) n -> r q a n", r=4)
-        w4s_dst = w4s_raw[:].bitcast(I32).rearrange("p (a n) -> p a n", a=2)
-        for r in range(4):
-            nc.gpsimd.dma_start(w4s_dst[r:P:32], w4s_src[r])
+        nc.gpsimd.memset(w4s_raw[32:64, :].bitcast(I32), 0)
+        nc.gpsimd.memset(w4s_raw[64:P, :].bitcast(I32), 0)
+        nc.gpsimd.memset(w4s[:].bitcast(I32), 0)
         nc.vector.memset(warm[:, 0:1], 1.0)
         nc.scalar.activation(warm[:, 1:2], warm[:, 0:1], ACT.Abs_reciprocal_sqrt)
         for i in range(8):
             nc.gpsimd.memset(win[i][:, PAIRS:], 0.0)
 
-        def load_w1(a, b):
-            for u in range(2):
-                c0 = PASS * b + PASS // 2 * u
-                nc.sync.dma_start(
-                    w1raw[a, b, u][:],
-                    w1[PASS * a : PASS * (a + 1), c0 : c0 + PASS // 2].rearrange("(p j) c -> p j c", j=PACK),
-                )
+        def load_w1(a, b, pieces=1):
+            src = w1[PASS * a : PASS * (a + 1), PASS * b : PASS * (b + 1)].rearrange("(p j) c -> p j c", j=PACK)
+            step = PACK // pieces
+            for j in range(0, PACK, step):
+                nc.sync.dma_start(w1raw[a, b][:, j : j + step, :], src[:, j : j + step, :])
 
         def load_rest(i):
             b, t = divmod(i, PACK)
@@ -99,18 +99,19 @@ def tile_list_polygraph_arousal_scorer_kernel(
             w4w_raw[:].bitcast(I32).rearrange("p (a n) -> p a n", a=2),
             w4_words.bitcast(I32).rearrange("a p n -> p a n"),
         )
-        load_tab(0)
         nc.sync.dma_start(offs_t[:], offs)
+        nc.sync.dma_start(w4s_raw[0:32, :].bitcast(I32), w4_scales.bitcast(I32).rearrange("a q n -> (a q) n"))
         nc.sync.dma_start(pos1_t[:], pos1)
         nc.sync.dma_start(pos2_t[:], pos2)
+        load_tab(0)
         nc.sync.dma_start(pos3_t[:], pos3)
         load_w1(0, 0)
         tabs_src = tab_scales.bitcast(I32)
         tabs_dst = tabs[:].bitcast(I32)
         for q in range(4):
             nc.sync.dma_start(tabs_dst[32 * q : 32 * q + 8, :], tabs_src[:, 4 * q : 4 * q + 4, :])
-        load_tab(1)
         load_w1(1, 0)
+        load_tab(1)
         load_rest(0)
         load_rest(1)
         load_w1(0, 1)
@@ -122,40 +123,60 @@ def tile_list_polygraph_arousal_scorer_kernel(
             load_rest(i)
 
         nc.vector.tensor_copy(
-            w4w[:].rearrange("p (g t q e) -> p g q t e", g=4, t=PACK, e=2),
-            w4w_raw[:].rearrange("p (g q t e) -> p g q t e", g=4, t=PACK, e=2),
+            w4w[:].bitcast(U16).rearrange("p (g t q) -> p g t q", g=4, t=PACK),
+            w4w_raw[:].bitcast(U16).rearrange("p (g q t) -> p g t q", g=4, t=PACK),
         )
+
         nc.vector.tensor_copy(
-            w4s[:].rearrange("p (g t q) -> p g q t", g=4, t=PACK),
-            w4s_raw[:].rearrange("p (g q t) -> p g q t", g=4, t=PACK),
+            w4s_dealt[:].rearrange("p (b t q) -> p b t q", b=2, t=PACK),
+            w4s_raw[:].rearrange("p (b q t) -> p b t q", b=2, t=PACK),
         )
+        for a in range(2):
+            for r in range(4):
+                nc.sync.dma_start(
+                    w4s[r:P:32, H * a : H * (a + 1)].bitcast(I32),
+                    w4s_dealt[16 * a + r : 16 * (a + 1) : 4, :].bitcast(I32),
+                )
 
-        def gather_words(a):
-            nc.vector.tensor_copy(vw[a][:], tabw[a][:].bitcast(U32).indirect(offs_t[:]))
+        def gather_words(a, j0, j1):
+            nc.vector.tensor_copy(vw[a][:, j0:j1], tabw[a][:].bitcast(U32).indirect(offs_t[:, j0 // 16 : j1 // 16]))
 
-        def quantize_w1(a, b, copies):
+        def quantize_w1(a, b, on_scalar):
             grouped = ring2.tile([P, PASS * PACK], BF16, name="grouped", align_bytes=64)
-            view = grouped[:].rearrange("p (t m j) -> p m j t", t=PACK, j=PACK)
-            for u in range(2):
-                copies[u](view[:, 64 * u : 64 * (u + 1)], w1raw[a, b, u][:].rearrange("p j (m t) -> p m j t", t=PACK))
+            dst = grouped[:].rearrange("p (t m j) -> p m t j", t=PACK, j=PACK)
+            src = w1raw[a, b][:].rearrange("p j (m t) -> p m t j", t=PACK)
+            nc.scalar.copy(dst[:, :on_scalar], src[:, :on_scalar])
+            if on_scalar < P:
+                nc.vector.tensor_copy(dst[:, on_scalar:], src[:, on_scalar:])
             nc.vector.quantize_mx(w1c[a, b][:].bitcast(FP8X4), w1s[a, b][:], grouped[:])
 
-        def make_h(i):
+        accs = {}
+        done = set()
+
+        def h_pass(i, u, a):
             b, t = divmod(i, PACK)
             cols = slice(P * t, P * (t + 1))
+            js = slice(BANK * u, BANK * (u + 1))
+            done.add((i, u, a))
+            if a == 0:
+                accs[i, u] = psum.tile([P, BANK], F32, name="acc", tag="bank%d" % ((2 * i + u) % 8))
+            nc.tensor.matmul_mx(
+                accs[i, u][:],
+                lhsT=w1c[a, b][:, cols].bitcast(FP8X4),
+                lhsT_scale=w1s[a, b][:, cols],
+                rhs=vw[a][:, js].bitcast(FP8X4),
+                rhs_scale=vs[4 * a : P, js],
+                start=(a == 0),
+                stop=(a == 1),
+            )
+
+        def make_h(i):
             for u in range(2):
-                acc = psum.tile([P, BANK], F32, name="acc", tag="bank%d" % ((2 * i + u) % 8))
                 js = slice(BANK * u, BANK * (u + 1))
                 for a in range(2):
-                    nc.tensor.matmul_mx(
-                        acc[:],
-                        lhsT=w1c[a, b][:, cols].bitcast(FP8X4),
-                        lhsT_scale=w1s[a, b][:, cols],
-                        rhs=vw[a][:, js].bitcast(FP8X4),
-                        rhs_scale=vs[4 * a : P, js],
-                        start=(a == 0),
-                        stop=(a == 1),
-                    )
+                    if (i, u, a) not in done:
+                        h_pass(i, u, a)
+                acc = accs[i, u]
                 if i in V_ADDS:
                     nc.vector.tensor_tensor(h_t[i][:, js], acc[:], rest_t[i][:, js], ALU.add)
                 else:
@@ -169,16 +190,16 @@ def tile_list_polygraph_arousal_scorer_kernel(
         def gather_pairs(i, m0, m1):
             t = i % PACK
             ls = slice(m0 // 16, m1 // 16)
-            nc.vector.tensor_copy(g1[:, t, m0:m1], h_t[i][:].indirect(pos1_t[:, ls]))
-            nc.vector.tensor_copy(g2[:, t, m0:m1], h_t[i][:].indirect(pos2_t[:, ls]))
+            nc.vector.tensor_copy(g1[:, t, : m1 - m0], h_t[i][:].indirect(pos1_t[:, ls]))
+            nc.vector.tensor_copy(g2[:, t, : m1 - m0], h_t[i][:].indirect(pos2_t[:, ls]))
 
         def make_x(b, m0, m1):
             n = m1 - m0
             xi = keep.tile([P, n * PACK], BF16, name="xi", tag="xi%d_%d" % (b, m0), align_bytes=64)
             nc.vector.tensor_tensor(
                 xi[:].rearrange("p (c i t) -> p c t i", t=PACK, i=4),
-                g1[:, :, m0:m1].rearrange("p t (c i) -> p c t i", i=4),
-                g2[:, :, m0:m1].rearrange("p t (c i) -> p c t i", i=4),
+                g1[:, :, :n].rearrange("p t (c i) -> p c t i", i=4),
+                g2[:, :, :n].rearrange("p t (c i) -> p c t i", i=4),
                 ALU.min,
             )
             nc.vector.quantize_mx(xc[b][:, m0:m1].bitcast(FP8X4), xs[b][:, m0:m1], xi[:])
@@ -213,24 +234,24 @@ def tile_list_polygraph_arousal_scorer_kernel(
         def finish(i):
             b, t = divmod(i, PACK)
             rows = out[PASS * b : PASS * (b + 1), :].rearrange("(p t) j -> t p j", t=PACK)
-            for u in range(2):
-                js = slice(BANK * u, BANK * (u + 1))
-                res = h_t[i][:, js]
-                picked = win[i][:].indirect(pos3_t[:, 32 * u : 32 * (u + 1)])
-                if i in V_FINAL:
-                    nc.vector.tensor_tensor(res, picked, rest_t[i][:, js], ALU.add)
-                    nc.sync.dma_start(rows[t][:, js], res)
-                else:
-                    nc.vector.tensor_copy(res, picked)
-                    nc.gpsimd.tensor_tensor(rest_t[i][:, js], res, rest_t[i][:, js], ALU.add)
-                    nc.sync.dma_start(rows[t][:, js], rest_t[i][:, js])
+            cuts = (0, BANK, BANK + HALF, S) if i == 7 else (0, BANK, S)
+            for j0, j1 in zip(cuts, cuts[1:]):
+                picked = win[i][:].indirect(pos3_t[:, j0 // 16 : j1 // 16])
+                nc.vector.tensor_tensor(h_t[i][:, j0:j1], picked, rest_t[i][:, j0:j1], ALU.add)
+                nc.sync.dma_start(rows[t][:, j0:j1], h_t[i][:, j0:j1])
 
-        on_scalar = (nc.scalar.copy, nc.scalar.copy)
-        gather_words(0)
+        on_scalar = P
+        gather_words(0, 0, S)
         nc.vector.tensor_copy(vs[:], tabs[:].indirect(offs_t[:]))
         quantize_w1(0, 0, on_scalar)
-        gather_words(1)
-        quantize_w1(1, 0, (nc.scalar.copy, nc.vector.tensor_copy))
+        for i in range(PACK):
+            for u in range(2):
+                h_pass(i, u, 0)
+        quantize_w1(1, 0, on_scalar)
+        gather_words(1, 0, BANK)
+        gather_words(1, BANK, S)
+        for i in range(PACK):
+            h_pass(i, 0, 1)
         make_h(0)
         make_h(1)
         gather_pairs(0, 0, PAIRS)
@@ -247,7 +268,7 @@ def tile_list_polygraph_arousal_scorer_kernel(
         make_h(7)
         for i in range(4):
             scale_h(i)
-        for i in range(4, 8):
+        for i in (4, 5, 7, 6):
             gather_pairs(i, 0, HALF)
         make_x(1, 0, HALF)
         for i in range(4, 8):

@@ -22,7 +22,7 @@ PASS = P * PACK
 BANK = 512
 HALF = PAIRS // 2
 SPARE = 16
-V_ADDS = (0, 7)
+V_ADDS = ((0, 0), (0, 1), (6, 1), (7, 0), (7, 1))
 V_FINAL = (0, 1, 2, 3, 4, 5, 6, 7)
 
 
@@ -34,7 +34,6 @@ def tile_list_polygraph_arousal_scorer_kernel(
         keep = ctx.enter_context(tc.tile_pool(name="keep", bufs=1))
         ring2 = ctx.enter_context(tc.tile_pool(name="ring2", bufs=2))
         ring3 = ctx.enter_context(tc.tile_pool(name="ring3", bufs=3))
-        shared = ctx.enter_context(tc.tile_pool(name="shared", bufs=1))
         psum = ctx.enter_context(tc.psum_pool(name="psum", bufs=1))
 
         offs_t = keep.tile([P, S // 16], U16, name="offs_t")
@@ -50,19 +49,17 @@ def tile_list_polygraph_arousal_scorer_kernel(
         w4s = keep.tile([P, 2 * H], U8, name="w4s", align_bytes=64)
         w4w = keep.tile([P, 2 * 2 * H], U8, name="w4w", align_bytes=64)
         tabw = [keep.tile([P, T], I32, name="tabw%d" % a, align_bytes=64) for a in range(2)]
-        tabs = shared.tile([P, T], U8, name="tabs", align_bytes=64, offset=0)
+        tabs = keep.tile([P, T], U8, name="tabs", align_bytes=64)
         vw = [keep.tile([P, S], U32, name="vw%d" % a, align_bytes=64) for a in range(2)]
-        vs = keep.tile([P, S], U8, name="vs", align_bytes=64)
+        vs_rows = keep.tile([P, S], U8, name="vs_rows", align_bytes=64)
+        vs = [keep.tile([P, S], U8, name="vs%d" % a, align_bytes=64) for a in range(2)]
         w1raw = {}
         w1c = {}
         w1s = {}
         for b in range(2):
             for a in range(2):
                 w1raw[a, b] = keep.tile([P, PACK, PASS], F32, name="w1raw%d%d" % (a, b), align_bytes=64)
-                if (a, b) == (0, 0):
-                    w1c[a, b] = shared.tile([P, PASS], U32, name="w1c00", align_bytes=64, offset=2 * H)
-                else:
-                    w1c[a, b] = keep.tile([P, PASS], U32, name="w1c%d%d" % (a, b), align_bytes=64)
+                w1c[a, b] = keep.tile([P, PASS], U32, name="w1c%d%d" % (a, b), align_bytes=64)
                 w1s[a, b] = keep.tile([P, PASS], U8, name="w1s%d%d" % (a, b), align_bytes=64)
         rest_t = [keep.tile([P, S], F32, name="rest%d" % i) for i in range(8)]
         h_t = [keep.tile([P, S], F32, name="h%d" % i) for i in range(8)]
@@ -72,7 +69,10 @@ def tile_list_polygraph_arousal_scorer_kernel(
         xs = [keep.tile([P, PAIRS], U8, name="xs%d" % b, align_bytes=64) for b in range(2)]
         win = [keep.tile([P, PAIRS + SPARE], F32, name="win%d" % i) for i in range(8)]
 
-        nc.vector.memset(tabs[:].bitcast(I32), 0)
+        nc.vector.memset(tabs[32:64, :].bitcast(I32), 0)
+        nc.vector.memset(tabs[64:P, :].bitcast(I32), 0)
+        for a in range(2):
+            nc.gpsimd.memset(vs[a][:].bitcast(I32), 0)
         nc.gpsimd.memset(w4s_raw[32:64, :].bitcast(I32), 0)
         nc.gpsimd.memset(w4s_raw[64:P, :].bitcast(I32), 0)
         nc.gpsimd.memset(w4s[:].bitcast(I32), 0)
@@ -95,24 +95,20 @@ def tile_list_polygraph_arousal_scorer_kernel(
         def load_tab(a):
             nc.sync.dma_start(tabw[a][:], tab_words[a].rearrange("p n i -> p (n i)").bitcast(I32))
 
+        nc.sync.dma_start(offs_t[:], offs)
+        nc.sync.dma_start(tabs[0:32, :].bitcast(I32), tab_scales.bitcast(I32).rearrange("a q n -> (a q) n"))
         nc.sync.dma_start(
             w4w_raw[:].bitcast(I32).rearrange("p (a n) -> p a n", a=2),
             w4_words.bitcast(I32).rearrange("a p n -> p a n"),
         )
-        nc.sync.dma_start(offs_t[:], offs)
-        nc.sync.dma_start(w4s_raw[0:32, :].bitcast(I32), w4_scales.bitcast(I32).rearrange("a q n -> (a q) n"))
-        nc.sync.dma_start(pos1_t[:], pos1)
-        nc.sync.dma_start(pos2_t[:], pos2)
         load_tab(0)
-        nc.sync.dma_start(pos3_t[:], pos3)
+        nc.sync.dma_start(w4s_raw[0:32, :].bitcast(I32), w4_scales.bitcast(I32).rearrange("a q n -> (a q) n"))
         load_w1(0, 0)
-        tabs_src = tab_scales.bitcast(I32)
-        tabs_dst = tabs[:].bitcast(I32)
-        for q in range(4):
-            nc.sync.dma_start(tabs_dst[32 * q : 32 * q + 8, :], tabs_src[:, 4 * q : 4 * q + 4, :])
         load_w1(1, 0)
         load_tab(1)
         load_rest(0)
+        nc.sync.dma_start(pos1_t[:], pos1)
+        nc.sync.dma_start(pos2_t[:], pos2)
         load_rest(1)
         load_w1(0, 1)
         load_rest(2)
@@ -121,6 +117,12 @@ def tile_list_polygraph_arousal_scorer_kernel(
         nc.sync.dma_start(gain_t[:], gain.rearrange("(b p t) -> p b t", b=2, t=PACK))
         for i in range(4, 8):
             load_rest(i)
+        nc.sync.dma_start(pos3_t[:], pos3)
+
+        nc.vector.tensor_copy(vs_rows[:], tabs[:].indirect(offs_t[:]))
+        for a in range(2):
+            for r in range(4):
+                nc.gpsimd.dma_start(vs[a][r:P:32, :].bitcast(I32), vs_rows[16 * a + r : 16 * (a + 1) : 4, :].bitcast(I32))
 
         nc.vector.tensor_copy(
             w4w[:].bitcast(U16).rearrange("p (g t q) -> p g t q", g=4, t=PACK),
@@ -165,7 +167,7 @@ def tile_list_polygraph_arousal_scorer_kernel(
                 lhsT=w1c[a, b][:, cols].bitcast(FP8X4),
                 lhsT_scale=w1s[a, b][:, cols],
                 rhs=vw[a][:, js].bitcast(FP8X4),
-                rhs_scale=vs[4 * a : P, js],
+                rhs_scale=vs[a][:, js],
                 start=(a == 0),
                 stop=(a == 1),
             )
@@ -177,7 +179,7 @@ def tile_list_polygraph_arousal_scorer_kernel(
                     if (i, u, a) not in done:
                         h_pass(i, u, a)
                 acc = accs[i, u]
-                if i in V_ADDS:
+                if (i, u) in V_ADDS:
                     nc.vector.tensor_tensor(h_t[i][:, js], acc[:], rest_t[i][:, js], ALU.add)
                 else:
                     nc.scalar.copy(h_t[i][:, js], acc[:])
@@ -242,7 +244,6 @@ def tile_list_polygraph_arousal_scorer_kernel(
 
         on_scalar = P
         gather_words(0, 0, S)
-        nc.vector.tensor_copy(vs[:], tabs[:].indirect(offs_t[:]))
         quantize_w1(0, 0, on_scalar)
         for i in range(PACK):
             for u in range(2):
@@ -256,9 +257,9 @@ def tile_list_polygraph_arousal_scorer_kernel(
         make_h(1)
         gather_pairs(0, 0, PAIRS)
         make_h(2)
+        make_h(3)
         quantize_w1(0, 1, on_scalar)
         gather_pairs(1, 0, PAIRS)
-        make_h(3)
         quantize_w1(1, 1, on_scalar)
         gather_pairs(2, 0, PAIRS)
         for i in range(4, 7):

from contextlib import ExitStack

import concourse.mybir as mybir

K, H, T, S, PAIRS = 1024, 1024, 4096, 1024, 512
FLOPS = 2 * K * H * S + 2 * H * H * PAIRS

F32 = mybir.dt.float32
BF16 = mybir.dt.bfloat16
I32 = mybir.dt.int32
U32 = mybir.dt.uint32
U16 = mybir.dt.uint16
U8 = mybir.dt.uint8
FP8X4 = mybir.dt.float8_e4m3fn_x4
FP4X4 = mybir.dt.float4_e2m1fn_x4
ALU = mybir.AluOpType
ACT = mybir.ActivationFunctionType

P = 128
PACK = 4
PASS = P * PACK
BANK = 512
HALF = PAIRS // 2
SPARE = 16
V_ADDS = ((0, 0), (0, 1), (6, 1), (7, 0), (7, 1))
V_FINAL = (0, 1, 2, 3, 4, 5, 6, 7)


def tile_list_polygraph_arousal_scorer_kernel(
    tc, tab_words, tab_scales, offs, w1, rest, pos1, pos2, w4_words, w4_scales, pos3, gain, out
):
    nc = tc.nc
    with ExitStack() as ctx:
        keep = ctx.enter_context(tc.tile_pool(name="keep", bufs=1))
        ring2 = ctx.enter_context(tc.tile_pool(name="ring2", bufs=2))
        ring3 = ctx.enter_context(tc.tile_pool(name="ring3", bufs=3))
        psum = ctx.enter_context(tc.psum_pool(name="psum", bufs=1))

        offs_t = keep.tile([P, S // 16], U16, name="offs_t")
        pos1_t = keep.tile([P, PAIRS // 16], U16, name="pos1_t")
        pos2_t = keep.tile([P, PAIRS // 16], U16, name="pos2_t")
        pos3_t = keep.tile([P, S // 16], U16, name="pos3_t")
        gain_t = keep.tile([P, 2, PACK], F32, name="gain_t")
        warm = keep.tile([P, 2], F32, name="warm")

        w4w_raw = keep.tile([P, 2 * 2 * H], U8, name="w4w_raw", align_bytes=64)
        w4s_raw = keep.tile([P, H], U8, name="w4s_raw", align_bytes=64)
        w4s_dealt = keep.tile([P, H], U8, name="w4s_dealt", align_bytes=64)
        w4s = keep.tile([P, 2 * H], U8, name="w4s", align_bytes=64)
        w4w = keep.tile([P, 2 * 2 * H], U8, name="w4w", align_bytes=64)
        tabw = [keep.tile([P, T], I32, name="tabw%d" % a, align_bytes=64) for a in range(2)]
        tabs = keep.tile([P, T], U8, name="tabs", align_bytes=64)
        vw = [keep.tile([P, S], U32, name="vw%d" % a, align_bytes=64) for a in range(2)]
        vs_rows = keep.tile([P, S], U8, name="vs_rows", align_bytes=64)
        vs = [keep.tile([P, S], U8, name="vs%d" % a, align_bytes=64) for a in range(2)]
        w1raw = {}
        w1c = {}
        w1s = {}
        for b in range(2):
            for a in range(2):
                w1raw[a, b] = keep.tile([P, PACK, PASS], F32, name="w1raw%d%d" % (a, b), align_bytes=64)
                w1c[a, b] = keep.tile([P, PASS], U32, name="w1c%d%d" % (a, b), align_bytes=64)
                w1s[a, b] = keep.tile([P, PASS], U8, name="w1s%d%d" % (a, b), align_bytes=64)
        rest_t = [keep.tile([P, S], F32, name="rest%d" % i) for i in range(8)]
        h_t = [keep.tile([P, S], F32, name="h%d" % i) for i in range(8)]
        g1 = keep.tile([P, PACK, PAIRS], F32, name="g1")
        g2 = keep.tile([P, PACK, PAIRS], F32, name="g2")
        xc = [keep.tile([P, PAIRS], U32, name="xc%d" % b, align_bytes=64) for b in range(2)]
        xs = [keep.tile([P, PAIRS], U8, name="xs%d" % b, align_bytes=64) for b in range(2)]
        win = [keep.tile([P, PAIRS + SPARE], F32, name="win%d" % i) for i in range(8)]

        nc.vector.memset(tabs[32:64, :].bitcast(I32), 0)
        nc.vector.memset(tabs[64:P, :].bitcast(I32), 0)
        for a in range(2):
            nc.gpsimd.memset(vs[a][:].bitcast(I32), 0)
        nc.gpsimd.memset(w4s_raw[32:64, :].bitcast(I32), 0)
        nc.gpsimd.memset(w4s_raw[64:P, :].bitcast(I32), 0)
        nc.gpsimd.memset(w4s[:].bitcast(I32), 0)
        nc.vector.memset(warm[:, 0:1], 1.0)
        nc.scalar.activation(warm[:, 1:2], warm[:, 0:1], ACT.Abs_reciprocal_sqrt)
        for i in range(8):
            nc.gpsimd.memset(win[i][:, PAIRS:], 0.0)

        def load_w1(a, b, pieces=1):
            src = w1[PASS * a : PASS * (a + 1), PASS * b : PASS * (b + 1)].rearrange("(p j) c -> p j c", j=PACK)
            step = PACK // pieces
            for j in range(0, PACK, step):
                nc.sync.dma_start(w1raw[a, b][:, j : j + step, :], src[:, j : j + step, :])

        def load_rest(i):
            b, t = divmod(i, PACK)
            rows = rest[PASS * b : PASS * (b + 1), :].rearrange("(p t) j -> t p j", t=PACK)
            nc.sync.dma_start(rest_t[i][:], rows[t])

        def load_tab(a):
            nc.sync.dma_start(tabw[a][:], tab_words[a].rearrange("p n i -> p (n i)").bitcast(I32))

        nc.sync.dma_start(offs_t[:], offs)
        nc.sync.dma_start(tabs[0:32, :].bitcast(I32), tab_scales.bitcast(I32).rearrange("a q n -> (a q) n"))
        nc.sync.dma_start(
            w4w_raw[:].bitcast(I32).rearrange("p (a n) -> p a n", a=2),
            w4_words.bitcast(I32).rearrange("a p n -> p a n"),
        )
        load_tab(0)
        nc.sync.dma_start(w4s_raw[0:32, :].bitcast(I32), w4_scales.bitcast(I32).rearrange("a q n -> (a q) n"))
        load_w1(0, 0)
        load_w1(1, 0)
        load_tab(1)
        load_rest(0)
        nc.sync.dma_start(pos1_t[:], pos1)
        nc.sync.dma_start(pos2_t[:], pos2)
        load_rest(1)
        load_w1(0, 1)
        load_rest(2)
        load_w1(1, 1)
        load_rest(3)
        nc.sync.dma_start(gain_t[:], gain.rearrange("(b p t) -> p b t", b=2, t=PACK))
        for i in range(4, 8):
            load_rest(i)
        nc.sync.dma_start(pos3_t[:], pos3)

        nc.vector.tensor_copy(vs_rows[:], tabs[:].indirect(offs_t[:]))
        for a in range(2):
            for r in range(4):
                nc.gpsimd.dma_start(vs[a][r:P:32, :].bitcast(I32), vs_rows[16 * a + r : 16 * (a + 1) : 4, :].bitcast(I32))

        nc.vector.tensor_copy(
            w4w[:].bitcast(U16).rearrange("p (g t q) -> p g t q", g=4, t=PACK),
            w4w_raw[:].bitcast(U16).rearrange("p (g q t) -> p g t q", g=4, t=PACK),
        )

        nc.vector.tensor_copy(
            w4s_dealt[:].rearrange("p (b t q) -> p b t q", b=2, t=PACK),
            w4s_raw[:].rearrange("p (b q t) -> p b t q", b=2, t=PACK),
        )
        for a in range(2):
            for r in range(4):
                nc.sync.dma_start(
                    w4s[r:P:32, H * a : H * (a + 1)].bitcast(I32),
                    w4s_dealt[16 * a + r : 16 * (a + 1) : 4, :].bitcast(I32),
                )

        def gather_words(a, j0, j1):
            nc.vector.tensor_copy(vw[a][:, j0:j1], tabw[a][:].bitcast(U32).indirect(offs_t[:, j0 // 16 : j1 // 16]))

        def quantize_w1(a, b, on_scalar):
            grouped = ring2.tile([P, PASS * PACK], BF16, name="grouped", align_bytes=64)
            dst = grouped[:].rearrange("p (t m j) -> p m t j", t=PACK, j=PACK)
            src = w1raw[a, b][:].rearrange("p j (m t) -> p m t j", t=PACK)
            nc.scalar.copy(dst[:, :on_scalar], src[:, :on_scalar])
            if on_scalar < P:
                nc.vector.tensor_copy(dst[:, on_scalar:], src[:, on_scalar:])
            nc.vector.quantize_mx(w1c[a, b][:].bitcast(FP8X4), w1s[a, b][:], grouped[:])

        accs = {}
        done = set()

        def h_pass(i, u, a):
            b, t = divmod(i, PACK)
            cols = slice(P * t, P * (t + 1))
            js = slice(BANK * u, BANK * (u + 1))
            done.add((i, u, a))
            if a == 0:
                accs[i, u] = psum.tile([P, BANK], F32, name="acc", tag="bank%d" % ((2 * i + u) % 8))
            nc.tensor.matmul_mx(
                accs[i, u][:],
                lhsT=w1c[a, b][:, cols].bitcast(FP8X4),
                lhsT_scale=w1s[a, b][:, cols],
                rhs=vw[a][:, js].bitcast(FP8X4),
                rhs_scale=vs[a][:, js],
                start=(a == 0),
                stop=(a == 1),
            )

        def make_h(i):
            for u in range(2):
                js = slice(BANK * u, BANK * (u + 1))
                for a in range(2):
                    if (i, u, a) not in done:
                        h_pass(i, u, a)
                acc = accs[i, u]
                if (i, u) in V_ADDS:
                    nc.vector.tensor_tensor(h_t[i][:, js], acc[:], rest_t[i][:, js], ALU.add)
                else:
                    nc.scalar.copy(h_t[i][:, js], acc[:])
                    nc.gpsimd.tensor_tensor(h_t[i][:, js], h_t[i][:, js], rest_t[i][:, js], ALU.add)

        def scale_h(i):
            b, t = divmod(i, PACK)
            nc.scalar.activation(rest_t[i][:], h_t[i][:], ACT.Copy, scale=gain_t[:, b, t : t + 1])

        def gather_pairs(i, m0, m1):
            t = i % PACK
            ls = slice(m0 // 16, m1 // 16)
            nc.vector.tensor_copy(g1[:, t, : m1 - m0], h_t[i][:].indirect(pos1_t[:, ls]))
            nc.vector.tensor_copy(g2[:, t, : m1 - m0], h_t[i][:].indirect(pos2_t[:, ls]))

        def make_x(b, m0, m1):
            n = m1 - m0
            xi = keep.tile([P, n * PACK], BF16, name="xi", tag="xi%d_%d" % (b, m0), align_bytes=64)
            nc.vector.tensor_tensor(
                xi[:].rearrange("p (c i t) -> p c t i", t=PACK, i=4),
                g1[:, :, :n].rearrange("p t (c i) -> p c t i", i=4),
                g2[:, :, :n].rearrange("p t (c i) -> p c t i", i=4),
                ALU.min,
            )
            nc.vector.quantize_mx(xc[b][:, m0:m1].bitcast(FP8X4), xs[b][:, m0:m1], xi[:])

        def scores(half, pair):
            acc = psum.tile([P, 2, HALF], F32, name="acc2", tag="bank%d" % (4 * half + pair))
            for v in range(2):
                i = 2 * pair + v
                for c in range(HALF // P):
                    ms = slice(HALF * half + P * c, HALF * half + P * (c + 1))
                    for a in range(2):
                        col = H * a + P * i
                        nc.tensor.matmul_mx(
                            acc[:, v, P * c : P * (c + 1)],
                            lhsT=w4w[:, 2 * col : 2 * (col + P)].bitcast(FP4X4),
                            lhsT_scale=w4s[:, col : col + P],
                            rhs=xc[a][:, ms].bitcast(FP8X4),
                            rhs_scale=xs[a][:, ms],
                            start=(a == 0),
                            stop=(a == 1),
                        )
            mag = ring2.tile([P, 2, HALF], F32, name="mag")
            root = ring2.tile([P, 2, HALF], F32, name="root")
            inv = ring3.tile([P, 2, HALF], F32, name="inv")
            nc.scalar.activation(mag[:], acc[:], ACT.Abs)
            nc.scalar.activation(root[:], mag[:], ACT.Abs_reciprocal_sqrt, bias=1.0)
            nc.scalar.activation(inv[:], root[:], ACT.Square)
            for v in range(2):
                i = 2 * pair + v
                nc.vector.tensor_tensor(win[i][:, HALF * half : HALF * (half + 1)], acc[:, v, :], inv[:, v, :], ALU.mult)

        def finish(i):
            b, t = divmod(i, PACK)
            rows = out[PASS * b : PASS * (b + 1), :].rearrange("(p t) j -> t p j", t=PACK)
            cuts = (0, BANK, BANK + HALF, S) if i == 7 else (0, BANK, S)
            for j0, j1 in zip(cuts, cuts[1:]):
                picked = win[i][:].indirect(pos3_t[:, j0 // 16 : j1 // 16])
                nc.vector.tensor_tensor(h_t[i][:, j0:j1], picked, rest_t[i][:, j0:j1], ALU.add)
                nc.sync.dma_start(rows[t][:, j0:j1], h_t[i][:, j0:j1])

        on_scalar = P
        gather_words(0, 0, S)
        quantize_w1(0, 0, on_scalar)
        for i in range(PACK):
            for u in range(2):
                h_pass(i, u, 0)
        quantize_w1(1, 0, on_scalar)
        gather_words(1, 0, BANK)
        gather_words(1, BANK, S)
        for i in range(PACK):
            h_pass(i, 0, 1)
        make_h(0)
        make_h(1)
        gather_pairs(0, 0, PAIRS)
        make_h(2)
        make_h(3)
        quantize_w1(0, 1, on_scalar)
        gather_pairs(1, 0, PAIRS)
        quantize_w1(1, 1, on_scalar)
        gather_pairs(2, 0, PAIRS)
        for i in range(4, 7):
            make_h(i)
        gather_pairs(3, 0, PAIRS)
        make_x(0, 0, PAIRS)
        make_h(7)
        for i in range(4):
            scale_h(i)
        for i in (4, 5, 7, 6):
            gather_pairs(i, 0, HALF)
        make_x(1, 0, HALF)
        for i in range(4, 8):
            gather_pairs(i, HALF, PAIRS)
        for pair in range(4):
            scores(0, pair)
        make_x(1, HALF, PAIRS)
        for pair in range(4):
            scores(1, pair)
            scale_h(4 + pair)
            finish(2 * pair)
            finish(2 * pair + 1)
